import numpy as np
import ml_dtypes


def mxq(x, axis, fmt="e4m3"):
    dtype, down = {"e4m3": (ml_dtypes.float8_e4m3fn, 7), "e5m2": (ml_dtypes.float8_e5m2, 14)}[fmt]
    v = np.moveaxis(np.asarray(x, np.float32).astype(ml_dtypes.bfloat16).astype(np.float64), axis, -1)
    blocks = v.reshape(v.shape[:-1] + (-1, 32))
    amax = np.abs(blocks).max(-1, keepdims=True)
    byte = np.maximum(np.where(amax > 0, np.frexp(amax)[1] - 1 + 127, 0) - down, 1)
    scale = np.exp2(byte - 127.0)
    codes = (blocks / scale).astype(np.float32).astype(dtype).astype(np.float64)
    return np.moveaxis((codes * scale).reshape(v.shape), -1, axis)


WIDE = False


def mx_kscale(k):
    if not WIDE:
        return np.ones(k)
    levels = np.array([30, -30])
    if k % 512:
        return np.exp2(np.random.permutation(np.resize(levels, k // 32))).repeat(32)
    a = np.empty((k // 512, 16))
    for p in range(k // 512):
        a[p, :8] = np.random.permutation(np.resize(levels, 8))
        for g in range(8):
            far = levels[np.abs(levels - a[p, g]) >= 10]
            a[p, g + 8] = far[np.random.randint(len(far))]
    return np.exp2(a.ravel()).repeat(32)


def f64(x):
    return np.asarray(x).astype(np.float64)


def striped(idx):
    return np.tile(np.asarray(idx).reshape(-1, 16).T, (8, 1)).astype(np.uint16)


def unstriped(offs):
    return offs[:16].T.reshape(-1).astype(np.int64)


E2M1 = np.array([0.0, 0.5, 1.0, 1.5, 2.0, 3.0, 4.0, 6.0, -0.0, -0.5, -1.0, -1.5, -2.0, -3.0, -4.0, -6.0])


def pack_weight(w, fmt):
    k, n = w.shape
    w = f64(np.asarray(w, np.float32).astype(ml_dtypes.bfloat16)).reshape(k // 32, 32, n)
    amax = np.abs(w).max(1)
    if fmt in ("e4m3", "e5m2"):
        byte = np.frexp(amax)[1] - 1 + 127 - (7 if fmt == "e4m3" else 14)
    else:
        mant, ex = np.frexp(amax / 6.0)
        byte = np.where(mant > 0.5, ex, ex - 1) + 127
    byte = np.clip(np.where(amax > 0, byte, 1), 1, 254)
    scaled = (w * np.exp2(127.0 - byte)[:, None, :]).reshape(k, n).astype(np.float32)
    by_word = np.ascontiguousarray(scaled.reshape(k // 512, 128, 4, n).transpose(0, 1, 3, 2))
    if fmt in ("e4m3", "e5m2"):
        words = by_word.astype(ml_dtypes.float8_e4m3fn if fmt == "e4m3" else ml_dtypes.float8_e5m2).view(np.uint8)
    else:
        c = by_word.astype(ml_dtypes.float4_e2m1fn).view(np.uint8) & 0xF
        words = (c[..., 0::2] | (c[..., 1::2] << 4)).reshape(k // 512, 128, 2 * n)
    return np.ascontiguousarray(words), np.ascontiguousarray(byte.astype(np.uint8).reshape(k // 512, 16, n))


def unpack_weight(words, scales, fmt):
    g, _, n = scales.shape
    words = np.ascontiguousarray(words).reshape(g, 128, n, -1)
    if fmt in ("e4m3", "e5m2"):
        vals = words.view(ml_dtypes.float8_e4m3fn if fmt == "e4m3" else ml_dtypes.float8_e5m2).astype(np.float64)
    else:
        nib = np.empty((g, 128, n, 4), np.uint8)
        nib[..., 0::2] = words & 0xF
        nib[..., 1::2] = words >> 4
        vals = E2M1[nib]
    vals = vals * np.repeat(np.exp2(scales.astype(np.float64) - 127.0), 8, axis=1)[..., None]
    return vals.transpose(0, 1, 3, 2).reshape(g * 512, n)


K, T, J, R, O, N = 512, 512, 256, 512, 128, 256


def setup_inputs():
    n = np.random.standard_normal
    idx = np.random.permutation(T)[:J]
    idx2 = np.random.permutation(J)[:O]
    idx3 = np.random.permutation(J)[:O]
    fk = mx_kscale(K)
    fr = mx_kscale(R)
    wp = pack_weight(n((K, R)) * 1 / np.sqrt(K) * fk[:, None] * fr, "e2m1")
    wbp = pack_weight(n((R, N)) * 1 / np.sqrt(R) / fr[:, None], "e5m2")
    return {
        "xf": (n((K, T))).astype(np.float32),
        "ow": (n((K, J)) * 0.7).astype(np.float32),
        "fk": (np.random.uniform(0.5, 2.0, (K, 1)) / fk[:, None]).astype(np.float32),
        "w_words": wp[0],
        "w_scales": wp[1],
        "wb_words": wbp[0],
        "wb_scales": wbp[1],
        "bi": (np.random.uniform(-0.5, 0.5, (1, N))).astype(np.float32),
        "offs": striped(idx),
        "offs2": striped(idx2),
        "offs3": striped(idx3),
    }


def reference(xf, ow, fk, w_words, w_scales, wb_words, wb_scales, bi, offs, offs2, offs3):
    idx = unstriped(offs)
    idx2 = unstriped(offs2)
    idx3 = unstriped(offs3)
    wu = unpack_weight(w_words, w_scales, "e2m1")
    wbu = unpack_weight(wb_words, wb_scales, "e5m2")
    u = (f64(xf)[:, idx] - f64(ow)) * f64(fk)
    uq = mxq(u, 0, "e4m3")
    a = wu.T @ uq
    hid = np.abs(a[:, idx2] - 0.5 * a[:, idx3])
    hidq = mxq(hid, 0, "e5m2")
    p = hidq.T @ wbu
    ea = np.exp(0.7 * p + f64(bi))
    y = 256.0 * ea / np.sum(ea, axis=1, keepdims=True)
    return y

@@ -1,0 +1,168 @@
+from contextlib import ExitStack
+
+import concourse.mybir as mybir
+
+K, T, J, R, O, N = 512, 512, 256, 512, 128, 256
+FLOPS = 2 * K * R * J + 2 * R * O * N
+
+F32 = mybir.dt.float32
+BF16 = mybir.dt.bfloat16
+I32 = mybir.dt.int32
+U32 = mybir.dt.uint32
+U16 = mybir.dt.uint16
+U8 = mybir.dt.uint8
+E4M3X4 = mybir.dt.float8_e4m3fn_x4
+E5M2X4 = mybir.dt.float8_e5m2_x4
+E2M1X4 = mybir.dt.float4_e2m1fn_x4
+ACT = mybir.ActivationFunctionType
+ALU = mybir.AluOpType
+AX = mybir.AxisListType
+
+P = 128
+PACK = 4
+
+
+def load_scale_rows(queue, plane, scales):
+    for q in range(4):
+        queue.dma_start(out=plane[32 * q : 32 * q + 4, :].bitcast(I32), in_=scales[0, 4 * q : 4 * q + 4, :].bitcast(I32))
+
+
+def tile_list_looks_offsetpicks_farther_rowshares_kernel(
+    tc, xf, ow, fk, w_words, w_scales, wb_words, wb_scales, bi, offs, offs2, offs3, out
+):
+    nc = tc.nc
+    with ExitStack() as ctx:
+        lists = ctx.enter_context(tc.tile_pool(name="lists", bufs=1))
+        sb = ctx.enter_context(tc.tile_pool(name="sb", bufs=1))
+        ps = ctx.enter_context(tc.psum_pool(name="ps", bufs=1))
+
+        l1 = lists.tile([P, J // 16], U16, name="l1")
+        l2 = lists.tile([P, O // 16], U16, name="l2")
+        l3 = lists.tile([P, O // 16], U16, name="l3")
+
+        w_raw = sb.tile([P, 2 * R], U8, name="w_raw", align_bytes=64)
+        ws_raw = sb.tile([P, R], U8, name="ws_raw", align_bytes=64)
+        w_codes = sb.tile([P, 2 * R], U8, name="w_codes", align_bytes=64)
+        w_plane = sb.tile([P, R], U8, name="w_plane", align_bytes=64)
+        wb_codes = sb.tile([P, N], U32, name="wb_codes", align_bytes=64)
+        wb_plane = sb.tile([P, N], U8, name="wb_plane", align_bytes=64)
+        fk_sb = sb.tile([P, PACK], F32, name="fk_sb")
+        bias = sb.tile([P, N], F32, name="bias")
+        x_pl = [sb.tile([P, T], F32, name=f"x{i}") for i in range(PACK)]
+        o_pl = [sb.tile([P, J], F32, name=f"o{i}") for i in range(PACK)]
+
+        nc.vector.memset(ws_raw[:].bitcast(I32), 0)
+        nc.vector.memset(wb_plane[:].bitcast(I32), 0)
+        load_scale_rows(nc.scalar, ws_raw, w_scales)
+        nc.gpsimd.dma_start(out=fk_sb[:], in_=fk.rearrange("(p i) o -> p (i o)", i=PACK))
+
+        xv = xf.rearrange("(p i) t -> p i t", i=PACK)
+        ov = ow.rearrange("(p i) j -> p i j", i=PACK)
+        nc.sync.dma_start(l1[:], offs)
+        for i in range(PACK):
+            nc.sync.dma_start(out=x_pl[i][:], in_=xv[:, i, :])
+        for i in range(PACK):
+            nc.sync.dma_start(out=o_pl[i][:], in_=ov[:, i, :])
+        nc.sync.dma_start(out=w_raw[:].bitcast(I32), in_=w_words[0].bitcast(I32))
+        nc.sync.dma_start(l2[:], offs2)
+        nc.sync.dma_start(l3[:], offs3)
+        nc.sync.dma_start(out=wb_codes[:].bitcast(I32), in_=wb_words[0].rearrange("p n t -> p (n t)").bitcast(I32))
+        load_scale_rows(nc.sync, wb_plane, wb_scales)
+        nc.sync.dma_start(out=bias[:], in_=bi.rearrange("o n -> (o n)").partition_broadcast(P))
+
+        nc.vector.tensor_copy(
+            out=w_plane[:].rearrange("p (t m) -> p t m", t=PACK),
+            in_=ws_raw[:].rearrange("p (m t) -> p t m", t=PACK),
+        )
+
+        half = J // 2
+        halves = [(0, half), (half, J)]
+        xs = [sb.tile([P, J], F32, name=f"xs{i}") for i in range(PACK)]
+        for i in range(PACK):
+            xg = sb.tile([P, J], F32, name=f"xg{i}")
+            if i == PACK - 1:
+                nc.vector.tensor_copy(xg[:, 0:half], x_pl[i][:].indirect(l1[:, 0 : half // 16]))
+                nc.scalar.activation(out=xg[:, half:J], in_=x_pl[i][:].indirect(l1[:, half // 16 : J // 16]), func=ACT.Copy)
+            elif i % 2 == 0:
+                nc.scalar.activation(out=xg[:], in_=x_pl[i][:].indirect(l1[:]), func=ACT.Copy)
+            else:
+                nc.vector.tensor_copy(xg[:], x_pl[i][:].indirect(l1[:]))
+            nc.vector.tensor_scalar(out=xs[i][:], in0=xg[:], scalar1=fk_sb[:, i : i + 1], scalar2=None, op0=ALU.mult)
+        un = sb.tile([P, PACK, J], BF16, name="un", align_bytes=64)
+        for i in range(PACK):
+            for j0, j1 in ([(0, J)] if i < PACK - 1 else halves):
+                nc.vector.scalar_tensor_tensor(
+                    out=un[:, i, j0:j1], in0=o_pl[i][:, j0:j1], scalar=fk_sb[:, i : i + 1], in1=xs[i][:, j0:j1],
+                    op0=ALU.mult, op1=ALU.subtract,
+                )
+        u = sb.tile([P, J, PACK], BF16, name="u", align_bytes=64)
+        u_codes = sb.tile([P, J], U32, name="u_codes", align_bytes=64)
+        u_plane = sb.tile([P, J], U8, name="u_plane", align_bytes=64)
+        for j0, j1 in halves:
+            nc.vector.tensor_copy(out=u[:, j0:j1, :], in_=un[:, :, j0:j1].rearrange("p i j -> p j i"))
+        for j0, j1 in halves:
+            nc.vector.quantize_mx(
+                out=u_codes[:, j0:j1].bitcast(E4M3X4),
+                scales=u_plane[:, j0:j1],
+                in_=u[:, j0:j1, :].rearrange("p j i -> p (j i)"),
+            )
+        nc.scalar.copy(
+            out=w_codes[:].bitcast(U16).rearrange("p (t m) -> p t m", t=PACK),
+            in_=w_raw[:].bitcast(U16).rearrange("p (m t) -> p t m", t=PACK),
+        )
+
+        dd = sb.tile([P, PACK, O], F32, name="dd")
+        a_sb = [sb.tile([P, J], F32, name=f"a{t}") for t in range(PACK)]
+        for t in range(PACK):
+            a_ps = ps.tile([P, J], F32, name=f"a_ps{t}")
+            nc.tensor.matmul_mx(
+                out=a_ps[:],
+                lhsT=w_codes[:, 2 * P * t : 2 * P * (t + 1)].bitcast(E2M1X4),
+                lhsT_scale=w_plane[:, P * t : P * (t + 1)],
+                rhs=u_codes[:].bitcast(E4M3X4),
+                rhs_scale=u_plane[:],
+                start=True,
+                stop=True,
+            )
+            if t < 2:
+                nc.scalar.copy(out=a_sb[t][:], in_=a_ps[:])
+            else:
+                nc.vector.tensor_copy(out=a_sb[t][:], in_=a_ps[:])
+        for t in range(PACK):
+            h = sb.tile([P, O], F32, name=f"h{t}")
+            nc.scalar.activation(out=h[:], in_=a_sb[t][:].indirect(l3[:]), func=ACT.Copy, scale=0.5)
+            nc.vector.tensor_tensor(dd[:, t, :], a_sb[t][:].indirect(l2[:]), h[:], ALU.subtract)
+
+        hid = sb.tile([P, O, PACK], BF16, name="hid", align_bytes=64)
+        ddv = dd[:].rearrange("p t o -> p o t")
+        oh = O // 2
+        nc.scalar.activation(out=hid[:, 0:oh, :], in_=ddv[:, 0:oh, :], func=ACT.Abs)
+        nc.vector.scalar_tensor_tensor(
+            out=hid[:, oh:O, :], in0=ddv[:, oh:O, :], scalar=-1.0, in1=ddv[:, oh:O, :], op0=ALU.mult, op1=ALU.max
+        )
+        h_codes = sb.tile([P, O], U32, name="h_codes", align_bytes=64)
+        h_plane = sb.tile([P, O], U8, name="h_plane", align_bytes=64)
+        nc.vector.quantize_mx(out=h_codes[:].bitcast(E5M2X4), scales=h_plane[:], in_=hid[:].rearrange("p o t -> p (o t)"))
+
+        p_ps = ps.tile([P, N], F32, name="p_ps")
+        nc.tensor.matmul_mx(
+            out=p_ps[:],
+            lhsT=h_codes[:].bitcast(E5M2X4),
+            lhsT_scale=h_plane[:],
+            rhs=wb_codes[:].bitcast(E5M2X4),
+            rhs_scale=wb_plane[:],
+            start=True,
+            stop=True,
+        )
+        z = sb.tile([P, N], F32, name="z")
+        nc.vector.scalar_tensor_tensor(out=z[:], in0=p_ps[:], scalar=0.7, in1=bias[:], op0=ALU.mult, op1=ALU.add)
+        neg_top = sb.tile([P, 1], F32, name="neg_top")
+        nc.vector.reduce_max(out=neg_top[:], in_=z[:], axis=AX.X, negate=True)
+        e = sb.tile([P, N], F32, name="e")
+        total = sb.tile([P, 1], F32, name="total")
+        nc.scalar.activation(out=e[:], in_=z[:], func=ACT.Exp, bias=neg_top[:], accum_out=total[:])
+        inv = sb.tile([P, 1], F32, name="inv")
+        nc.vector.reciprocal(out=inv[:], in_=total[:])
+        y = sb.tile([P, N], F32, name="y")
+        nc.vector.tensor_scalar(out=y[:], in0=e[:], scalar1=inv[:], scalar2=float(N), op0=ALU.mult, op1=ALU.mult)
+        nc.sync.dma_start(out=out, in_=y[:])

@@ -22,9 +22,16 @@ P = 128
 PACK = 4
 
 
-def load_scale_rows(queue, plane, scales):
+def load_scale_rows(queues, plane, scales):
     for q in range(4):
-        queue.dma_start(out=plane[32 * q : 32 * q + 4, :].bitcast(I32), in_=scales[0, 4 * q : 4 * q + 4, :].bitcast(I32))
+        queues[q].dma_start(out=plane[32 * q : 32 * q + 4, :].bitcast(I32), in_=scales[0, 4 * q : 4 * q + 4, :].bitcast(I32))
+
+
+def load_repeated_rows(queue, plane, scales, q):
+    rows = scales[0, 4 * q : 4 * q + 4, :].bitcast(I32)
+    queue.dma_start(
+        out=plane[32 * q : 32 * q + 32, :].bitcast(I32), in_=rows.rearrange("r c -> (r c)").partition_broadcast(8)
+    )
 
 
 def tile_list_looks_offsetpicks_farther_rowshares_kernel(
@@ -49,28 +56,38 @@ def tile_list_looks_offsetpicks_farther_rowshares_kernel(
         fk_sb = sb.tile([P, PACK], F32, name="fk_sb")
         bias = sb.tile([P, N], F32, name="bias")
         x_pl = [sb.tile([P, T], F32, name=f"x{i}") for i in range(PACK)]
-        o_pl = [sb.tile([P, J], F32, name=f"o{i}") for i in range(PACK)]
+        o0 = sb.tile([P, J], F32, name="o0")
+        o1 = sb.tile([P, J], F32, name="o1")
+        o23 = sb.tile([P, 2, J], F32, name="o23")
+        o_pl = [o0[:], o1[:], o23[:, 0, :], o23[:, 1, :]]
 
-        nc.vector.memset(ws_raw[:].bitcast(I32), 0)
         nc.vector.memset(wb_plane[:].bitcast(I32), 0)
-        load_scale_rows(nc.scalar, ws_raw, w_scales)
-        nc.gpsimd.dma_start(out=fk_sb[:], in_=fk.rearrange("(p i) o -> p (i o)", i=PACK))
+        nc.sync.dma_start(l1[:], offs)
+        nc.scalar.dma_start(out=fk_sb[:], in_=fk.rearrange("(p i) o -> p (i o)", i=PACK))
+        load_repeated_rows(nc.scalar, ws_raw, w_scales, 0)
+        load_repeated_rows(nc.scalar, ws_raw, w_scales, 1)
+        neg_fk = sb.tile([P, PACK], F32, name="neg_fk")
+        nc.scalar.activation(out=neg_fk[:], in_=fk_sb[:], func=ACT.Copy, scale=-1.0)
 
         xv = xf.rearrange("(p i) t -> p i t", i=PACK)
         ov = ow.rearrange("(p i) j -> p i j", i=PACK)
-        nc.sync.dma_start(l1[:], offs)
-        for i in range(PACK):
-            nc.sync.dma_start(out=x_pl[i][:], in_=xv[:, i, :])
-        for i in range(PACK):
-            nc.sync.dma_start(out=o_pl[i][:], in_=ov[:, i, :])
+        nc.sync.dma_start(out=x_pl[0][:], in_=xv[:, 0, :])
+        nc.sync.dma_start(out=x_pl[1][:], in_=xv[:, 1, :])
+        nc.sync.dma_start(out=o0[:], in_=ov[:, 0, :])
+        nc.sync.dma_start(out=x_pl[2][:], in_=xv[:, 2, :])
+        load_repeated_rows(nc.sync, ws_raw, w_scales, 2)
+        load_repeated_rows(nc.sync, ws_raw, w_scales, 3)
+        nc.sync.dma_start(out=x_pl[3][:], in_=xv[:, 3, :])
+        nc.sync.dma_start(out=o1[:], in_=ov[:, 1, :])
+        nc.sync.dma_start(out=o23[:], in_=ov[:, 2:4, :])
         nc.sync.dma_start(out=w_raw[:].bitcast(I32), in_=w_words[0].bitcast(I32))
         nc.sync.dma_start(l2[:], offs2)
         nc.sync.dma_start(l3[:], offs3)
         nc.sync.dma_start(out=wb_codes[:].bitcast(I32), in_=wb_words[0].rearrange("p n t -> p (n t)").bitcast(I32))
-        load_scale_rows(nc.sync, wb_plane, wb_scales)
+        load_scale_rows([nc.sync] * 4, wb_plane, wb_scales)
         nc.sync.dma_start(out=bias[:], in_=bi.rearrange("o n -> (o n)").partition_broadcast(P))
 
-        nc.vector.tensor_copy(
+        nc.gpsimd.tensor_copy(
             out=w_plane[:].rearrange("p (t m) -> p t m", t=PACK),
             in_=ws_raw[:].rearrange("p (m t) -> p t m", t=PACK),
         )
@@ -83,55 +100,66 @@ def tile_list_looks_offsetpicks_farther_rowshares_kernel(
             if i == PACK - 1:
                 nc.vector.tensor_copy(xg[:, 0:half], x_pl[i][:].indirect(l1[:, 0 : half // 16]))
                 nc.scalar.activation(out=xg[:, half:J], in_=x_pl[i][:].indirect(l1[:, half // 16 : J // 16]), func=ACT.Copy)
-            elif i % 2 == 0:
+            elif i > 0:
                 nc.scalar.activation(out=xg[:], in_=x_pl[i][:].indirect(l1[:]), func=ACT.Copy)
             else:
                 nc.vector.tensor_copy(xg[:], x_pl[i][:].indirect(l1[:]))
-            nc.vector.tensor_scalar(out=xs[i][:], in0=xg[:], scalar1=fk_sb[:, i : i + 1], scalar2=None, op0=ALU.mult)
+            if i < PACK - 1:
+                nc.vector.tensor_scalar(out=xs[i][:], in0=xg[:], scalar1=fk_sb[:, i : i + 1], scalar2=None, op0=ALU.mult)
+            else:
+                nc.scalar.activation(out=xs[i][:], in_=xg[:], func=ACT.Copy, scale=fk_sb[:, i : i + 1])
         un = sb.tile([P, PACK, J], BF16, name="un", align_bytes=64)
         for i in range(PACK):
             for j0, j1 in ([(0, J)] if i < PACK - 1 else halves):
                 nc.vector.scalar_tensor_tensor(
-                    out=un[:, i, j0:j1], in0=o_pl[i][:, j0:j1], scalar=fk_sb[:, i : i + 1], in1=xs[i][:, j0:j1],
-                    op0=ALU.mult, op1=ALU.subtract,
+                    out=un[:, i, j0:j1], in0=o_pl[i][:, j0:j1], scalar=neg_fk[:, i : i + 1], in1=xs[i][:, j0:j1],
+                    op0=ALU.mult, op1=ALU.add,
                 )
+        nc.scalar.copy(
+            out=w_codes[:].bitcast(U16).rearrange("p (t m) -> p t m", t=PACK),
+            in_=w_raw[:].bitcast(U16).rearrange("p (m t) -> p t m", t=PACK),
+        )
         u = sb.tile([P, J, PACK], BF16, name="u", align_bytes=64)
         u_codes = sb.tile([P, J], U32, name="u_codes", align_bytes=64)
         u_plane = sb.tile([P, J], U8, name="u_plane", align_bytes=64)
-        for j0, j1 in halves:
+        cut = 3 * J // 4
+        for j0, j1 in [(0, half), (half, cut)]:
             nc.vector.tensor_copy(out=u[:, j0:j1, :], in_=un[:, :, j0:j1].rearrange("p i j -> p j i"))
+        nc.scalar.copy(out=u[:, cut:J, :], in_=un[:, :, cut:J].rearrange("p i j -> p j i"))
         for j0, j1 in halves:
             nc.vector.quantize_mx(
                 out=u_codes[:, j0:j1].bitcast(E4M3X4),
                 scales=u_plane[:, j0:j1],
                 in_=u[:, j0:j1, :].rearrange("p j i -> p (j i)"),
             )
-        nc.scalar.copy(
-            out=w_codes[:].bitcast(U16).rearrange("p (t m) -> p t m", t=PACK),
-            in_=w_raw[:].bitcast(U16).rearrange("p (m t) -> p t m", t=PACK),
-        )
 
         dd = sb.tile([P, PACK, O], F32, name="dd")
         a_sb = [sb.tile([P, J], F32, name=f"a{t}") for t in range(PACK)]
-        for t in range(PACK):
-            a_ps = ps.tile([P, J], F32, name=f"a_ps{t}")
+        pieces = [(0, 0, half), (1, 0, half), (0, half, J), (1, half, J), (2, 0, J), (3, 0, J)]
+        for t, j0, j1 in pieces:
+            a_ps = ps.tile([P, j1 - j0], F32, name=f"a_ps{t}_{j0}")
             nc.tensor.matmul_mx(
                 out=a_ps[:],
                 lhsT=w_codes[:, 2 * P * t : 2 * P * (t + 1)].bitcast(E2M1X4),
                 lhsT_scale=w_plane[:, P * t : P * (t + 1)],
-                rhs=u_codes[:].bitcast(E4M3X4),
-                rhs_scale=u_plane[:],
+                rhs=u_codes[:, j0:j1].bitcast(E4M3X4),
+                rhs_scale=u_plane[:, j0:j1],
                 start=True,
                 stop=True,
             )
             if t < 2:
-                nc.scalar.copy(out=a_sb[t][:], in_=a_ps[:])
+                nc.scalar.copy(out=a_sb[t][:, j0:j1], in_=a_ps[:])
             else:
-                nc.vector.tensor_copy(out=a_sb[t][:], in_=a_ps[:])
+                nc.vector.tensor_copy(out=a_sb[t][:, j0:j1], in_=a_ps[:])
         for t in range(PACK):
             h = sb.tile([P, O], F32, name=f"h{t}")
             nc.scalar.activation(out=h[:], in_=a_sb[t][:].indirect(l3[:]), func=ACT.Copy, scale=0.5)
-            nc.vector.tensor_tensor(dd[:, t, :], a_sb[t][:].indirect(l2[:]), h[:], ALU.subtract)
+            if t < PACK - 1:
+                nc.vector.tensor_tensor(dd[:, t, :], a_sb[t][:].indirect(l2[:]), h[:], ALU.subtract)
+            else:
+                g = sb.tile([P, O], F32, name="g")
+                nc.scalar.activation(out=g[:], in_=a_sb[t][:].indirect(l2[:]), func=ACT.Copy)
+                nc.vector.tensor_tensor(dd[:, t, :], g[:], h[:], ALU.subtract)
 
         hid = sb.tile([P, O, PACK], BF16, name="hid", align_bytes=64)
         ddv = dd[:].rearrange("p t o -> p o t")
@@ -163,6 +191,8 @@ def tile_list_looks_offsetpicks_farther_rowshares_kernel(
         nc.scalar.activation(out=e[:], in_=z[:], func=ACT.Exp, bias=neg_top[:], accum_out=total[:])
         inv = sb.tile([P, 1], F32, name="inv")
         nc.vector.reciprocal(out=inv[:], in_=total[:])
-        y = sb.tile([P, N], F32, name="y")
-        nc.vector.tensor_scalar(out=y[:], in0=e[:], scalar1=inv[:], scalar2=float(N), op0=ALU.mult, op1=ALU.mult)
-        nc.sync.dma_start(out=out, in_=y[:])
+        for queue, n0 in [(nc.sync, 0), (nc.scalar, N // 2)]:
+            cols = slice(n0, n0 + N // 2)
+            y = sb.tile([P, N // 2], F32, name=f"y{n0}")
+            nc.vector.tensor_scalar(out=y[:], in0=e[:, cols], scalar1=inv[:], scalar2=float(N), op0=ALU.mult, op1=ALU.mult)
+            queue.dma_start(out=out[:, cols], in_=y[:])

@@ -64,7 +64,7 @@ def tile_list_looks_offsetpicks_farther_rowshares_kernel(
         nc.vector.memset(wb_plane[:].bitcast(I32), 0)
         nc.sync.dma_start(l1[:], offs)
         nc.scalar.dma_start(out=fk_sb[:], in_=fk.rearrange("(p i) o -> p (i o)", i=PACK))
-        load_repeated_rows(nc.scalar, ws_raw, w_scales, 0)
+        load_repeated_rows(nc.sync, ws_raw, w_scales, 0)
         load_repeated_rows(nc.scalar, ws_raw, w_scales, 1)
         neg_fk = sb.tile([P, PACK], F32, name="neg_fk")
         nc.scalar.activation(out=neg_fk[:], in_=fk_sb[:], func=ACT.Copy, scale=-1.0)

@@ -22,16 +22,9 @@ P = 128
 PACK = 4
 
 
-def load_scale_rows(queues, plane, scales):
-    for q in range(4):
-        queues[q].dma_start(out=plane[32 * q : 32 * q + 4, :].bitcast(I32), in_=scales[0, 4 * q : 4 * q + 4, :].bitcast(I32))
-
-
-def load_repeated_rows(queue, plane, scales, q):
-    rows = scales[0, 4 * q : 4 * q + 4, :].bitcast(I32)
-    queue.dma_start(
-        out=plane[32 * q : 32 * q + 32, :].bitcast(I32), in_=rows.rearrange("r c -> (r c)").partition_broadcast(8)
-    )
+def load_scale_rows(queue, plane, scales, quadrants):
+    for q in quadrants:
+        queue.dma_start(out=plane[32 * q : 32 * q + 4, :].bitcast(I32), in_=scales[0, 4 * q : 4 * q + 4, :].bitcast(I32))
 
 
 def tile_list_looks_offsetpicks_farther_rowshares_kernel(
@@ -61,11 +54,11 @@ def tile_list_looks_offsetpicks_farther_rowshares_kernel(
         o23 = sb.tile([P, 2, J], F32, name="o23")
         o_pl = [o0[:], o1[:], o23[:, 0, :], o23[:, 1, :]]
 
+        nc.vector.memset(ws_raw[:].bitcast(I32), 0)
         nc.vector.memset(wb_plane[:].bitcast(I32), 0)
         nc.sync.dma_start(l1[:], offs)
         nc.scalar.dma_start(out=fk_sb[:], in_=fk.rearrange("(p i) o -> p (i o)", i=PACK))
-        load_repeated_rows(nc.sync, ws_raw, w_scales, 0)
-        load_repeated_rows(nc.scalar, ws_raw, w_scales, 1)
+        load_scale_rows(nc.scalar, ws_raw, w_scales, (0, 1))
         neg_fk = sb.tile([P, PACK], F32, name="neg_fk")
         nc.scalar.activation(out=neg_fk[:], in_=fk_sb[:], func=ACT.Copy, scale=-1.0)
 
@@ -75,8 +68,7 @@ def tile_list_looks_offsetpicks_farther_rowshares_kernel(
         nc.sync.dma_start(out=x_pl[1][:], in_=xv[:, 1, :])
         nc.sync.dma_start(out=o0[:], in_=ov[:, 0, :])
         nc.sync.dma_start(out=x_pl[2][:], in_=xv[:, 2, :])
-        load_repeated_rows(nc.sync, ws_raw, w_scales, 2)
-        load_repeated_rows(nc.sync, ws_raw, w_scales, 3)
+        load_scale_rows(nc.scalar, ws_raw, w_scales, (2, 3))
         nc.sync.dma_start(out=x_pl[3][:], in_=xv[:, 3, :])
         nc.sync.dma_start(out=o1[:], in_=ov[:, 1, :])
         nc.sync.dma_start(out=o23[:], in_=ov[:, 2:4, :])
@@ -84,7 +76,7 @@ def tile_list_looks_offsetpicks_farther_rowshares_kernel(
         nc.sync.dma_start(l2[:], offs2)
         nc.sync.dma_start(l3[:], offs3)
         nc.sync.dma_start(out=wb_codes[:].bitcast(I32), in_=wb_words[0].rearrange("p n t -> p (n t)").bitcast(I32))
-        load_scale_rows([nc.sync] * 4, wb_plane, wb_scales)
+        load_scale_rows(nc.sync, wb_plane, wb_scales, range(4))
         nc.sync.dma_start(out=bias[:], in_=bi.rearrange("o n -> (o n)").partition_broadcast(P))
 
         nc.gpsimd.tensor_copy(

from contextlib import ExitStack

import concourse.mybir as mybir

K, T, J, R, O, N = 512, 512, 256, 512, 128, 256
FLOPS = 2 * K * R * J + 2 * R * O * N

F32 = mybir.dt.float32
BF16 = mybir.dt.bfloat16
I32 = mybir.dt.int32
U32 = mybir.dt.uint32
U16 = mybir.dt.uint16
U8 = mybir.dt.uint8
E4M3X4 = mybir.dt.float8_e4m3fn_x4
E5M2X4 = mybir.dt.float8_e5m2_x4
E2M1X4 = mybir.dt.float4_e2m1fn_x4
ACT = mybir.ActivationFunctionType
ALU = mybir.AluOpType
AX = mybir.AxisListType

P = 128
PACK = 4


def load_scale_rows(queue, plane, scales, quadrants):
    for q in quadrants:
        queue.dma_start(out=plane[32 * q : 32 * q + 4, :].bitcast(I32), in_=scales[0, 4 * q : 4 * q + 4, :].bitcast(I32))


def tile_list_looks_offsetpicks_farther_rowshares_kernel(
    tc, xf, ow, fk, w_words, w_scales, wb_words, wb_scales, bi, offs, offs2, offs3, out
):
    nc = tc.nc
    with ExitStack() as ctx:
        lists = ctx.enter_context(tc.tile_pool(name="lists", bufs=1))
        sb = ctx.enter_context(tc.tile_pool(name="sb", bufs=1))
        ps = ctx.enter_context(tc.psum_pool(name="ps", bufs=1))

        l1 = lists.tile([P, J // 16], U16, name="l1")
        l2 = lists.tile([P, O // 16], U16, name="l2")
        l3 = lists.tile([P, O // 16], U16, name="l3")

        w_raw = sb.tile([P, 2 * R], U8, name="w_raw", align_bytes=64)
        ws_raw = sb.tile([P, R], U8, name="ws_raw", align_bytes=64)
        w_codes = sb.tile([P, 2 * R], U8, name="w_codes", align_bytes=64)
        w_plane = sb.tile([P, R], U8, name="w_plane", align_bytes=64)
        wb_codes = sb.tile([P, N], U32, name="wb_codes", align_bytes=64)
        wb_plane = sb.tile([P, N], U8, name="wb_plane", align_bytes=64)
        fk_sb = sb.tile([P, PACK], F32, name="fk_sb")
        bias = sb.tile([P, N], F32, name="bias")
        x_pl = [sb.tile([P, T], F32, name=f"x{i}") for i in range(PACK)]
        o0 = sb.tile([P, J], F32, name="o0")
        o1 = sb.tile([P, J], F32, name="o1")
        o23 = sb.tile([P, 2, J], F32, name="o23")
        o_pl = [o0[:], o1[:], o23[:, 0, :], o23[:, 1, :]]

        nc.vector.memset(ws_raw[:].bitcast(I32), 0)
        nc.vector.memset(wb_plane[:].bitcast(I32), 0)
        nc.sync.dma_start(l1[:], offs)
        nc.scalar.dma_start(out=fk_sb[:], in_=fk.rearrange("(p i) o -> p (i o)", i=PACK))
        load_scale_rows(nc.scalar, ws_raw, w_scales, (0, 1))
        neg_fk = sb.tile([P, PACK], F32, name="neg_fk")
        nc.scalar.activation(out=neg_fk[:], in_=fk_sb[:], func=ACT.Copy, scale=-1.0)

        xv = xf.rearrange("(p i) t -> p i t", i=PACK)
        ov = ow.rearrange("(p i) j -> p i j", i=PACK)
        nc.sync.dma_start(out=x_pl[0][:], in_=xv[:, 0, :])
        nc.sync.dma_start(out=x_pl[1][:], in_=xv[:, 1, :])
        nc.sync.dma_start(out=o0[:], in_=ov[:, 0, :])
        nc.sync.dma_start(out=x_pl[2][:], in_=xv[:, 2, :])
        load_scale_rows(nc.scalar, ws_raw, w_scales, (2, 3))
        nc.sync.dma_start(out=x_pl[3][:], in_=xv[:, 3, :])
        nc.sync.dma_start(out=o1[:], in_=ov[:, 1, :])
        nc.sync.dma_start(out=o23[:], in_=ov[:, 2:4, :])
        nc.sync.dma_start(out=w_raw[:].bitcast(I32), in_=w_words[0].bitcast(I32))
        nc.sync.dma_start(l2[:], offs2)
        nc.sync.dma_start(l3[:], offs3)
        nc.sync.dma_start(out=wb_codes[:].bitcast(I32), in_=wb_words[0].rearrange("p n t -> p (n t)").bitcast(I32))
        load_scale_rows(nc.sync, wb_plane, wb_scales, range(4))
        nc.sync.dma_start(out=bias[:], in_=bi.rearrange("o n -> (o n)").partition_broadcast(P))

        nc.gpsimd.tensor_copy(
            out=w_plane[:].rearrange("p (t m) -> p t m", t=PACK),
            in_=ws_raw[:].rearrange("p (m t) -> p t m", t=PACK),
        )

        half = J // 2
        halves = [(0, half), (half, J)]
        xs = [sb.tile([P, J], F32, name=f"xs{i}") for i in range(PACK)]
        for i in range(PACK):
            xg = sb.tile([P, J], F32, name=f"xg{i}")
            if i == PACK - 1:
                nc.vector.tensor_copy(xg[:, 0:half], x_pl[i][:].indirect(l1[:, 0 : half // 16]))
                nc.scalar.activation(out=xg[:, half:J], in_=x_pl[i][:].indirect(l1[:, half // 16 : J // 16]), func=ACT.Copy)
            elif i > 0:
                nc.scalar.activation(out=xg[:], in_=x_pl[i][:].indirect(l1[:]), func=ACT.Copy)
            else:
                nc.vector.tensor_copy(xg[:], x_pl[i][:].indirect(l1[:]))
            if i < PACK - 1:
                nc.vector.tensor_scalar(out=xs[i][:], in0=xg[:], scalar1=fk_sb[:, i : i + 1], scalar2=None, op0=ALU.mult)
            else:
                nc.scalar.activation(out=xs[i][:], in_=xg[:], func=ACT.Copy, scale=fk_sb[:, i : i + 1])
        un = sb.tile([P, PACK, J], BF16, name="un", align_bytes=64)
        for i in range(PACK):
            for j0, j1 in ([(0, J)] if i < PACK - 1 else halves):
                nc.vector.scalar_tensor_tensor(
                    out=un[:, i, j0:j1], in0=o_pl[i][:, j0:j1], scalar=neg_fk[:, i : i + 1], in1=xs[i][:, j0:j1],
                    op0=ALU.mult, op1=ALU.add,
                )
        nc.scalar.copy(
            out=w_codes[:].bitcast(U16).rearrange("p (t m) -> p t m", t=PACK),
            in_=w_raw[:].bitcast(U16).rearrange("p (m t) -> p t m", t=PACK),
        )
        u = sb.tile([P, J, PACK], BF16, name="u", align_bytes=64)
        u_codes = sb.tile([P, J], U32, name="u_codes", align_bytes=64)
        u_plane = sb.tile([P, J], U8, name="u_plane", align_bytes=64)
        cut = 3 * J // 4
        for j0, j1 in [(0, half), (half, cut)]:
            nc.vector.tensor_copy(out=u[:, j0:j1, :], in_=un[:, :, j0:j1].rearrange("p i j -> p j i"))
        nc.scalar.copy(out=u[:, cut:J, :], in_=un[:, :, cut:J].rearrange("p i j -> p j i"))
        for j0, j1 in halves:
            nc.vector.quantize_mx(
                out=u_codes[:, j0:j1].bitcast(E4M3X4),
                scales=u_plane[:, j0:j1],
                in_=u[:, j0:j1, :].rearrange("p j i -> p (j i)"),
            )

        dd = sb.tile([P, PACK, O], F32, name="dd")
        a_sb = [sb.tile([P, J], F32, name=f"a{t}") for t in range(PACK)]
        pieces = [(0, 0, half), (1, 0, half), (0, half, J), (1, half, J), (2, 0, J), (3, 0, J)]
        for t, j0, j1 in pieces:
            a_ps = ps.tile([P, j1 - j0], F32, name=f"a_ps{t}_{j0}")
            nc.tensor.matmul_mx(
                out=a_ps[:],
                lhsT=w_codes[:, 2 * P * t : 2 * P * (t + 1)].bitcast(E2M1X4),
                lhsT_scale=w_plane[:, P * t : P * (t + 1)],
                rhs=u_codes[:, j0:j1].bitcast(E4M3X4),
                rhs_scale=u_plane[:, j0:j1],
                start=True,
                stop=True,
            )
            if t < 2:
                nc.scalar.copy(out=a_sb[t][:, j0:j1], in_=a_ps[:])
            else:
                nc.vector.tensor_copy(out=a_sb[t][:, j0:j1], in_=a_ps[:])
        for t in range(PACK):
            h = sb.tile([P, O], F32, name=f"h{t}")
            nc.scalar.activation(out=h[:], in_=a_sb[t][:].indirect(l3[:]), func=ACT.Copy, scale=0.5)
            if t < PACK - 1:
                nc.vector.tensor_tensor(dd[:, t, :], a_sb[t][:].indirect(l2[:]), h[:], ALU.subtract)
            else:
                g = sb.tile([P, O], F32, name="g")
                nc.scalar.activation(out=g[:], in_=a_sb[t][:].indirect(l2[:]), func=ACT.Copy)
                nc.vector.tensor_tensor(dd[:, t, :], g[:], h[:], ALU.subtract)

        hid = sb.tile([P, O, PACK], BF16, name="hid", align_bytes=64)
        ddv = dd[:].rearrange("p t o -> p o t")
        oh = O // 2
        nc.scalar.activation(out=hid[:, 0:oh, :], in_=ddv[:, 0:oh, :], func=ACT.Abs)
        nc.vector.scalar_tensor_tensor(
            out=hid[:, oh:O, :], in0=ddv[:, oh:O, :], scalar=-1.0, in1=ddv[:, oh:O, :], op0=ALU.mult, op1=ALU.max
        )
        h_codes = sb.tile([P, O], U32, name="h_codes", align_bytes=64)
        h_plane = sb.tile([P, O], U8, name="h_plane", align_bytes=64)
        nc.vector.quantize_mx(out=h_codes[:].bitcast(E5M2X4), scales=h_plane[:], in_=hid[:].rearrange("p o t -> p (o t)"))

        p_ps = ps.tile([P, N], F32, name="p_ps")
        nc.tensor.matmul_mx(
            out=p_ps[:],
            lhsT=h_codes[:].bitcast(E5M2X4),
            lhsT_scale=h_plane[:],
            rhs=wb_codes[:].bitcast(E5M2X4),
            rhs_scale=wb_plane[:],
            start=True,
            stop=True,
        )
        z = sb.tile([P, N], F32, name="z")
        nc.vector.scalar_tensor_tensor(out=z[:], in0=p_ps[:], scalar=0.7, in1=bias[:], op0=ALU.mult, op1=ALU.add)
        neg_top = sb.tile([P, 1], F32, name="neg_top")
        nc.vector.reduce_max(out=neg_top[:], in_=z[:], axis=AX.X, negate=True)
        e = sb.tile([P, N], F32, name="e")
        total = sb.tile([P, 1], F32, name="total")
        nc.scalar.activation(out=e[:], in_=z[:], func=ACT.Exp, bias=neg_top[:], accum_out=total[:])
        inv = sb.tile([P, 1], F32, name="inv")
        nc.vector.reciprocal(out=inv[:], in_=total[:])
        for queue, n0 in [(nc.sync, 0), (nc.scalar, N // 2)]:
            cols = slice(n0, n0 + N // 2)
            y = sb.tile([P, N // 2], F32, name=f"y{n0}")
            nc.vector.tensor_scalar(out=y[:], in0=e[:, cols], scalar1=inv[:], scalar2=float(N), op0=ALU.mult, op1=ALU.mult)
            queue.dma_start(out=out[:, cols], in_=y[:])
